import numpy as np
import ml_dtypes


def mxq(x, axis, fmt="e4m3"):
    dtype, down = {"e4m3": (ml_dtypes.float8_e4m3fn, 7), "e5m2": (ml_dtypes.float8_e5m2, 14)}[fmt]
    v = np.moveaxis(np.asarray(x, np.float32).astype(ml_dtypes.bfloat16).astype(np.float64), axis, -1)
    blocks = v.reshape(v.shape[:-1] + (-1, 32))
    amax = np.abs(blocks).max(-1, keepdims=True)
    byte = np.maximum(np.where(amax > 0, np.frexp(amax)[1] - 1 + 127, 0) - down, 1)
    scale = np.exp2(byte - 127.0)
    codes = (blocks / scale).astype(np.float32).astype(dtype).astype(np.float64)
    return np.moveaxis((codes * scale).reshape(v.shape), -1, axis)


WIDE = False


def mx_kscale(k):
    if not WIDE:
        return np.ones(k)
    levels = np.array([10, -10, 5, -5, 0])
    if k % 512:
        return np.exp2(np.random.permutation(np.resize(levels, k // 32))).repeat(32)
    a = np.empty((k // 512, 16))
    for p in range(k // 512):
        a[p, :8] = np.random.permutation(np.resize(levels, 8))
        for g in range(8):
            far = levels[np.abs(levels - a[p, g]) >= 10]
            a[p, g + 8] = far[np.random.randint(len(far))]
    return np.exp2(a.ravel()).repeat(32)


def f64(x):
    return np.asarray(x).astype(np.float64)


def striped(idx):
    return np.tile(idx.reshape(-1, 16).T, (8, 1)).astype(np.uint16)


def unstriped(offs):
    return offs[:16].T.reshape(-1).astype(np.int64)


K, T, E, C, N = 1024, 1024, 8, 128, 512


def by_expert(wq, xq):
    return np.concatenate([wq[e].T @ xq[:, e * C:(e + 1) * C] for e in range(E)], axis=1)


def setup_inputs():
    n = np.random.standard_normal
    s = mx_kscale(K)[:, None]
    return {
        "xT": (n((K, T)) * s).astype(np.float32),
        "w": (n((E, K, N)) / np.sqrt(K) / s[None]).astype(np.float32),
        "gate": np.tile(np.random.uniform(0.2, 1.0, E * C), (N, 1)).astype(np.float32),
        "offs": striped(np.random.permutation(T)[:E * C]),
    }


def reference(xT, w, gate, offs):
    idx = unstriped(offs)
    xq = mxq(f64(xT)[:, idx], 0, "e4m3")
    y = by_expert(mxq(f64(w), 1, "e4m3"), xq)
    out = np.zeros((N, T))
    out[:, idx] = f64(gate) * y
    return out

@@ -1,0 +1,173 @@
+from contextlib import ExitStack
+
+import concourse.mybir as mybir
+
+K, T, E, C, N = 1024, 1024, 8, 128, 512
+FLOPS = 2 * E * C * K * N
+BYTES = 4 * (K * T + E * K * N + E * C + N * T) + 2 * 128 * (E * C // 16)
+
+F32 = mybir.dt.float32
+BF16 = mybir.dt.bfloat16
+U32 = mybir.dt.uint32
+U16 = mybir.dt.uint16
+U8 = mybir.dt.uint8
+FP8X4 = mybir.dt.float8_e4m3fn_x4
+MULT = mybir.AluOpType.mult
+
+P = 128
+PACK = 4
+K_PASS = P * PACK
+PASSES = K // K_PASS
+BLOCKS = N // P
+COLS_PER_EXPERT = C // 16
+RAW_BUFS = 11
+
+
+def tile_routed_moe_kernel(tc, xT, w, gate, offs, out):
+    nc = tc.nc
+    with ExitStack() as ctx:
+        keep = ctx.enter_context(tc.tile_pool(name="keep", bufs=1))
+        rawp = ctx.enter_context(tc.tile_pool(name="rawp", bufs=RAW_BUFS))
+        bfp = ctx.enter_context(tc.tile_pool(name="bfp", bufs=5))
+        yp = ctx.enter_context(tc.tile_pool(name="yp", bufs=6))
+        psum = ctx.enter_context(tc.psum_pool(name="psum", bufs=2))
+
+        offsets = keep.tile([P, E * C // 16], U16, name="offsets")
+        gates = keep.tile([P, E * C], F32, name="gates")
+        x_codes = [keep.tile([P, T], U32, name=f"x_codes{g}", align_bytes=64) for g in range(PASSES)]
+        x_scales = keep.tile([P, T], U8, name="x_scales", align_bytes=64)
+        half = E * C // 2
+        s_codes = [[keep.tile([P, half], U32, name=f"s_codes{g}_{h}", align_bytes=64) for h in range(2)] for g in range(PASSES)]
+        s_scales = [keep.tile([P, half], U8, name=f"s_scales{h}", align_bytes=64) for h in range(2)]
+        w_codes = [[keep.tile([P, N], U32, name=f"w_codes{e}_{g}", align_bytes=64) for g in range(PASSES)] for e in range(E)]
+        w_scales = [[keep.tile([P, N], U8, name=f"w_scales{e}_{g}", align_bytes=64) for g in range(PASSES)] for e in range(E)]
+        windows = [keep.tile([P, T], F32, name=f"window{b}") for b in range(BLOCKS)]
+
+        nc.gpsimd.memset(x_scales[:], 0)
+
+        x_units = [("x", 0, 0, 256), ("x", 0, 256, 256), ("x", 0, 512, 512), ("x", 1, 0, 512), ("x", 1, 512, 512)]
+        w_units = [("w", e, g, 0, N) for e in range(E - 1) for g in range(PASSES)]
+        w_units += [("w", E - 1, g, c, N // 2) for c in (0, N // 2) for g in range(PASSES)]
+        units = x_units + w_units
+        raws = {}
+
+        def load(i):
+            unit = units[i]
+            if unit[0] == "x":
+                g, c0, width = unit[1:]
+                source = xT[g * K_PASS:(g + 1) * K_PASS, c0:c0 + width]
+            else:
+                e, g, c0, width = unit[1:]
+                source = w[e, g * K_PASS:(g + 1) * K_PASS, c0:c0 + width]
+            raw = rawp.tile([P, PACK, width], F32, name="raw")
+            nc.sync.dma_start(out=raw[:], in_=source.rearrange("(p j) n -> p j n", j=PACK))
+            raws[i] = raw
+            if i == 0:
+                nc.sync.dma_start(offsets[:], offs)
+            if i == len(x_units):
+                nc.sync.dma_start(out=gates[:], in_=gate[0:P, :])
+
+        def interleave(i, vector_columns):
+            width = units[i][-1]
+            raw = raws[i]
+            grouped = bfp.tile([P, width, PACK], BF16, name="grouped", align_bytes=64)
+            for c0, c1, copy in ((0, vector_columns, nc.vector.tensor_copy), (vector_columns, width, nc.scalar.copy)):
+                if c1 > c0:
+                    copy(
+                        out=grouped[:, c0:c1, :].rearrange("p (c i) j -> p c j i", i=4),
+                        in_=raw[:, :, c0:c1].rearrange("p j (c i) -> p c j i", i=4),
+                    )
+            return grouped
+
+        def quantise(i, grouped):
+            unit = units[i]
+            if unit[0] == "x":
+                g, c0, width = unit[1:]
+                codes, scales = x_codes[g][:, c0:c0 + width], x_scales[4 * g:P, c0:c0 + width]
+            else:
+                e, g, c0, width = unit[1:]
+                codes, scales = w_codes[e][g][:, c0:c0 + width], w_scales[e][g][:, c0:c0 + width]
+            nc.vector.quantize_mx(out=codes.bitcast(FP8X4), scales=scales, in_=grouped[:].rearrange("p n j -> p (n j)"))
+
+        def gather_codes(g, h):
+            n = half // 16
+            nc.vector.tensor_copy(s_codes[g][h][:], x_codes[g][:].indirect(offsets[:, h * n:(h + 1) * n]))
+
+        def gather_scales(h):
+            n = half // 16
+            nc.vector.tensor_copy(s_scales[h][:], x_scales[:].indirect(offsets[:, h * n:(h + 1) * n]))
+
+        banks = {}
+
+        def multiply(e, first, b):
+            if e == first:
+                banks[b] = psum.tile([P, 4 * C], F32, name=f"bank{b}")
+            h, s = divmod(e * C, half)
+            for g in range(PASSES):
+                nc.tensor.matmul_mx(
+                    out=banks[b][:, (e - first) * C:(e - first + 1) * C],
+                    lhsT=w_codes[e][g][:, b * P:(b + 1) * P].bitcast(FP8X4),
+                    lhsT_scale=w_scales[e][g][:, b * P:(b + 1) * P],
+                    rhs=s_codes[g][h][:, s:s + C].bitcast(FP8X4),
+                    rhs_scale=s_scales[h][4 * g:P, s:s + C],
+                    start=(g == 0),
+                    stop=(g == PASSES - 1),
+                )
+
+        def finish(first, count, b, bank):
+            n = count * C
+            y = yp.tile([P, n], F32, name="y")
+            nc.scalar.copy(out=y[:], in_=bank[:, 0:n])
+            o0 = first * COLS_PER_EXPERT
+            nc.vector.tensor_tensor(
+                windows[b][:].indirect(offsets[:, o0:o0 + n // 16]), y[:], gates[:, first * C:first * C + n], MULT
+            )
+
+        for i in range(RAW_BUFS):
+            load(i)
+        issued = RAW_BUFS
+
+        x_vector = (192, 192, 320, 128, 320)
+        groups = {0: (0, 2), 1: (0, 2), 2: (2, 2), 3: (2, 2), 4: (4, 2), 5: (4, 2), 6: (6, 1), 7: (7, 1)}
+        pending = []
+        for i, unit in enumerate(units):
+            share = x_vector[i] if unit[0] == "x" else 0
+            if i == len(units) - 1:
+                share = 128
+            grouped = interleave(i, share)
+            quantise(i, grouped)
+            if issued < len(units):
+                load(issued)
+                issued += 1
+            if unit[0] == "x":
+                if i == 2:
+                    gather_codes(0, 0)
+                if i == 4:
+                    gather_codes(1, 0)
+                    gather_scales(0)
+                continue
+            e, g, c0, width = unit[1:]
+            if e == 0 and g == 1:
+                gather_codes(0, 1)
+            if e == 1 and g == 0:
+                gather_codes(1, 1)
+            if e == 1 and g == 1:
+                gather_scales(1)
+            if g == PASSES - 1:
+                first, count = groups[e]
+                done = e == first + count - 1
+                todo = pending
+                pending = []
+                for b in range(c0 // P, (c0 + width) // P):
+                    multiply(e, first, b)
+                    if done:
+                        pending.append((first, count, b, banks[b]))
+                for item in todo:
+                    finish(*item)
+                    if item[0] == E - 1:
+                        b = item[2]
+                        nc.sync.dma_start(out=out[b * P:(b + 1) * P, :], in_=windows[b][:])
+        for item in pending:
+            finish(*item)
+            b = item[2]
+            nc.sync.dma_start(out=out[b * P:(b + 1) * P, :], in_=windows[b][:])

@@ -20,94 +20,75 @@ K_PASS = P * PACK
 PASSES = K // K_PASS
 BLOCKS = N // P
 COLS_PER_EXPERT = C // 16
-RAW_BUFS = 11
+LOADS_AHEAD = 11
+HALF = E * C // 2
 
 
 def tile_routed_moe_kernel(tc, xT, w, gate, offs, out):
     nc = tc.nc
     with ExitStack() as ctx:
         keep = ctx.enter_context(tc.tile_pool(name="keep", bufs=1))
-        rawp = ctx.enter_context(tc.tile_pool(name="rawp", bufs=RAW_BUFS))
-        bfp = ctx.enter_context(tc.tile_pool(name="bfp", bufs=5))
-        yp = ctx.enter_context(tc.tile_pool(name="yp", bufs=6))
+        rawp = ctx.enter_context(tc.tile_pool(name="rawp", bufs=LOADS_AHEAD))
+        bfp = ctx.enter_context(tc.tile_pool(name="bfp", bufs=9))
+        yp = ctx.enter_context(tc.tile_pool(name="yp", bufs=16))
         psum = ctx.enter_context(tc.psum_pool(name="psum", bufs=2))
 
         offsets = keep.tile([P, E * C // 16], U16, name="offsets")
         gates = keep.tile([P, E * C], F32, name="gates")
         x_codes = [keep.tile([P, T], U32, name=f"x_codes{g}", align_bytes=64) for g in range(PASSES)]
         x_scales = keep.tile([P, T], U8, name="x_scales", align_bytes=64)
-        half = E * C // 2
-        s_codes = [[keep.tile([P, half], U32, name=f"s_codes{g}_{h}", align_bytes=64) for h in range(2)] for g in range(PASSES)]
-        s_scales = [keep.tile([P, half], U8, name=f"s_scales{h}", align_bytes=64) for h in range(2)]
-        w_codes = [[keep.tile([P, N], U32, name=f"w_codes{e}_{g}", align_bytes=64) for g in range(PASSES)] for e in range(E)]
-        w_scales = [[keep.tile([P, N], U8, name=f"w_scales{e}_{g}", align_bytes=64) for g in range(PASSES)] for e in range(E)]
+        s_codes = [[keep.tile([P, HALF], U32, name=f"s_codes{g}_{h}", align_bytes=64) for h in range(2)] for g in range(PASSES)]
+        s_scales = [keep.tile([P, HALF], U8, name=f"s_scales{h}", align_bytes=64) for h in range(2)]
         windows = [keep.tile([P, T], F32, name=f"window{b}") for b in range(BLOCKS)]
 
         nc.gpsimd.memset(x_scales[:], 0)
 
-        x_units = [("x", 0, 0, 256), ("x", 0, 256, 256), ("x", 0, 512, 512), ("x", 1, 0, 512), ("x", 1, 512, 512)]
-        w_units = [("w", e, g, 0, N) for e in range(E - 1) for g in range(PASSES)]
-        w_units += [("w", E - 1, g, c, N // 2) for c in (0, N // 2) for g in range(PASSES)]
-        units = x_units + w_units
-        raws = {}
+        x_units = [(0, 0, 256, 256), (0, 256, 256, 256), (0, 512, 512, 320), (1, 0, 512, 0), (1, 512, 512, 320)]
+        w_parts = [(e, 0, N) for e in range(E - 1)] + [(E - 1, 0, N // 2), (E - 1, N // 2, N // 2)]
+        sources = [xT[g * K_PASS:(g + 1) * K_PASS, t0:t0 + n] for g, t0, n, v in x_units]
+        for e, c0, n in w_parts:
+            sources += [w[e, g * K_PASS:(g + 1) * K_PASS, c0:c0 + n] for g in range(PASSES)]
+        raws = []
 
-        def load(i):
-            unit = units[i]
-            if unit[0] == "x":
-                g, c0, width = unit[1:]
-                source = xT[g * K_PASS:(g + 1) * K_PASS, c0:c0 + width]
-            else:
-                e, g, c0, width = unit[1:]
-                source = w[e, g * K_PASS:(g + 1) * K_PASS, c0:c0 + width]
-            raw = rawp.tile([P, PACK, width], F32, name="raw")
-            nc.sync.dma_start(out=raw[:], in_=source.rearrange("(p j) n -> p j n", j=PACK))
-            raws[i] = raw
+        def load():
+            i = len(raws)
+            if i == len(sources):
+                return
+            raw = rawp.tile([P, PACK, sources[i].shape[1]], F32, name="raw")
+            nc.sync.dma_start(out=raw[:], in_=sources[i].rearrange("(p j) n -> p j n", j=PACK))
+            raws.append(raw)
             if i == 0:
                 nc.sync.dma_start(offsets[:], offs)
-            if i == len(x_units):
+            if i == len(x_units) + 2:
                 nc.sync.dma_start(out=gates[:], in_=gate[0:P, :])
 
-        def interleave(i, vector_columns):
-            width = units[i][-1]
-            raw = raws[i]
-            grouped = bfp.tile([P, width, PACK], BF16, name="grouped", align_bytes=64)
-            for c0, c1, copy in ((0, vector_columns, nc.vector.tensor_copy), (vector_columns, width, nc.scalar.copy)):
+        def interleave(raw, grouped, vector_columns):
+            width = raw.shape[2]
+            ends = (0, vector_columns, width)
+            for engine, c0, c1 in zip("vs", ends, ends[1:]):
                 if c1 > c0:
-                    copy(
-                        out=grouped[:, c0:c1, :].rearrange("p (c i) j -> p c j i", i=4),
-                        in_=raw[:, :, c0:c1].rearrange("p j (c i) -> p c j i", i=4),
-                    )
-            return grouped
-
-        def quantise(i, grouped):
-            unit = units[i]
-            if unit[0] == "x":
-                g, c0, width = unit[1:]
-                codes, scales = x_codes[g][:, c0:c0 + width], x_scales[4 * g:P, c0:c0 + width]
-            else:
-                e, g, c0, width = unit[1:]
-                codes, scales = w_codes[e][g][:, c0:c0 + width], w_scales[e][g][:, c0:c0 + width]
-            nc.vector.quantize_mx(out=codes.bitcast(FP8X4), scales=scales, in_=grouped[:].rearrange("p n j -> p (n j)"))
+                    dst = grouped[:, c0:c1, :].rearrange("p (c i) j -> p c j i", i=4)
+                    src = raw[:, :, c0:c1].rearrange("p j (c i) -> p c j i", i=4)
+                    if engine == "v":
+                        nc.vector.tensor_copy(out=dst, in_=src)
+                    elif engine == "s":
+                        nc.scalar.copy(out=dst, in_=src)
 
         def gather_codes(g, h):
-            n = half // 16
+            n = HALF // 16
             nc.vector.tensor_copy(s_codes[g][h][:], x_codes[g][:].indirect(offsets[:, h * n:(h + 1) * n]))
 
         def gather_scales(h):
-            n = half // 16
+            n = HALF // 16
             nc.vector.tensor_copy(s_scales[h][:], x_scales[:].indirect(offsets[:, h * n:(h + 1) * n]))
 
-        banks = {}
-
-        def multiply(e, first, b):
-            if e == first:
-                banks[b] = psum.tile([P, 4 * C], F32, name=f"bank{b}")
-            h, s = divmod(e * C, half)
+        def multiply(bank, e, first, w_codes, w_scales, b):
+            h, s = divmod(e * C, HALF)
             for g in range(PASSES):
                 nc.tensor.matmul_mx(
-                    out=banks[b][:, (e - first) * C:(e - first + 1) * C],
-                    lhsT=w_codes[e][g][:, b * P:(b + 1) * P].bitcast(FP8X4),
-                    lhsT_scale=w_scales[e][g][:, b * P:(b + 1) * P],
+                    out=bank[:, (e - first) * C:(e - first + 1) * C],
+                    lhsT=w_codes[:, g, b * P:(b + 1) * P].bitcast(FP8X4),
+                    lhsT_scale=w_scales[:, g, b * P:(b + 1) * P],
                     rhs=s_codes[g][h][:, s:s + C].bitcast(FP8X4),
                     rhs_scale=s_scales[h][4 * g:P, s:s + C],
                     start=(g == 0),
@@ -122,52 +103,54 @@ def tile_routed_moe_kernel(tc, xT, w, gate, offs, out):
             nc.vector.tensor_tensor(
                 windows[b][:].indirect(offsets[:, o0:o0 + n // 16]), y[:], gates[:, first * C:first * C + n], MULT
             )
+            if first + count == E:
+                nc.sync.dma_start(out=out[b * P:(b + 1) * P, :], in_=windows[b][:])
 
-        for i in range(RAW_BUFS):
-            load(i)
-        issued = RAW_BUFS
+        for i in range(LOADS_AHEAD):
+            load()
+        for i, (g, t0, n, v) in enumerate(x_units):
+            grouped = bfp.tile([P, n, PACK], BF16, tag="grouped", name="x_grouped", align_bytes=64)
+            interleave(raws[i], grouped, v)
+            nc.vector.quantize_mx(
+                out=x_codes[g][:, t0:t0 + n].bitcast(FP8X4),
+                scales=x_scales[4 * g:P, t0:t0 + n],
+                in_=grouped[:].rearrange("p n j -> p (n j)"),
+            )
+            load()
+            if t0 + n == T:
+                gather_codes(g, 0)
+                gather_codes(g, 1)
+        gather_scales(0)
+        gather_scales(1)
 
-        x_vector = (192, 192, 320, 128, 320)
-        groups = {0: (0, 2), 1: (0, 2), 2: (2, 2), 3: (2, 2), 4: (4, 2), 5: (4, 2), 6: (6, 1), 7: (7, 1)}
-        pending = []
-        for i, unit in enumerate(units):
-            share = x_vector[i] if unit[0] == "x" else 0
-            if i == len(units) - 1:
-                share = 128
-            grouped = interleave(i, share)
-            quantise(i, grouped)
-            if issued < len(units):
-                load(issued)
-                issued += 1
-            if unit[0] == "x":
-                if i == 2:
-                    gather_codes(0, 0)
-                if i == 4:
-                    gather_codes(1, 0)
-                    gather_scales(0)
-                continue
-            e, g, c0, width = unit[1:]
-            if e == 0 and g == 1:
-                gather_codes(0, 1)
-            if e == 1 and g == 0:
-                gather_codes(1, 1)
-            if e == 1 and g == 1:
-                gather_scales(1)
-            if g == PASSES - 1:
-                first, count = groups[e]
-                done = e == first + count - 1
-                todo = pending
-                pending = []
-                for b in range(c0 // P, (c0 + width) // P):
-                    multiply(e, first, b)
-                    if done:
-                        pending.append((first, count, b, banks[b]))
-                for item in todo:
-                    finish(*item)
-                    if item[0] == E - 1:
-                        b = item[2]
-                        nc.sync.dma_start(out=out[b * P:(b + 1) * P, :], in_=windows[b][:])
-        for item in pending:
+        groups = tuple((e, 1) for e in range(E))
+        group_of = {e: (first, count) for first, count in groups for e in range(first, first + count)}
+        vector_columns = {(e, 1): 160 for e in range(1, 7)}
+        banks = {}
+        waiting = []
+        for i, (e, c0, n) in enumerate(w_parts):
+            w_codes = keep.tile([P, PASSES, n], U32, name=f"w_codes{i}", align_bytes=64)
+            w_scales = keep.tile([P, PASSES, n], U8, name=f"w_scales{i}", align_bytes=64)
+            for g in range(PASSES):
+                grouped = bfp.tile([P, n, PACK], BF16, tag="grouped", name="w_grouped", align_bytes=64)
+                interleave(raws[len(x_units) + PASSES * i + g], grouped, vector_columns.get((i, g), 0))
+                nc.vector.quantize_mx(
+                    out=w_codes[:, g, :].bitcast(FP8X4),
+                    scales=w_scales[:, g, :],
+                    in_=grouped[:].rearrange("p n j -> p (n j)"),
+                )
+                load()
+            first, count = group_of[e]
+            ready = waiting
+            waiting = []
+            for b in range(n // P):
+                block = c0 // P + b
+                if e == first:
+                    banks[block] = psum.tile([P, count * C], F32, name=f"bank{block}")
+                multiply(banks[block], e, first, w_codes, w_scales, b)
+                if e == first + count - 1:
+                    waiting.append((first, count, block, banks[block]))
+            for item in ready:
+                finish(*item)
+        for item in waiting:
             finish(*item)
-            b = item[2]
-            nc.sync.dma_start(out=out[b * P:(b + 1) * P, :], in_=windows[b][:])

@@ -19,9 +19,9 @@ PACK = 4
 K_PASS = P * PACK
 PASSES = K // K_PASS
 BLOCKS = N // P
-COLS_PER_EXPERT = C // 16
-LOADS_AHEAD = 11
 HALF = E * C // 2
+LOADS_AHEAD = 10
+GATE_LOAD = 6
 
 
 def tile_routed_moe_kernel(tc, xT, w, gate, offs, out):
@@ -29,7 +29,7 @@ def tile_routed_moe_kernel(tc, xT, w, gate, offs, out):
     with ExitStack() as ctx:
         keep = ctx.enter_context(tc.tile_pool(name="keep", bufs=1))
         rawp = ctx.enter_context(tc.tile_pool(name="rawp", bufs=LOADS_AHEAD))
-        bfp = ctx.enter_context(tc.tile_pool(name="bfp", bufs=9))
+        bfp = ctx.enter_context(tc.tile_pool(name="bfp", bufs=10))
         yp = ctx.enter_context(tc.tile_pool(name="yp", bufs=16))
         psum = ctx.enter_context(tc.psum_pool(name="psum", bufs=2))
 
@@ -43,114 +43,108 @@ def tile_routed_moe_kernel(tc, xT, w, gate, offs, out):
 
         nc.gpsimd.memset(x_scales[:], 0)
 
-        x_units = [(0, 0, 256, 256), (0, 256, 256, 256), (0, 512, 512, 320), (1, 0, 512, 0), (1, 512, 512, 320)]
-        w_parts = [(e, 0, N) for e in range(E - 1)] + [(E - 1, 0, N // 2), (E - 1, N // 2, N // 2)]
-        sources = [xT[g * K_PASS:(g + 1) * K_PASS, t0:t0 + n] for g, t0, n, v in x_units]
-        for e, c0, n in w_parts:
-            sources += [w[e, g * K_PASS:(g + 1) * K_PASS, c0:c0 + n] for g in range(PASSES)]
+        w_parts = [(e, 0, N) for e in range(E - 1)] + [(E - 1, c, P) for c in range(0, N, P)]
+        w_units = [("w", i, g) for i in range(len(w_parts)) for g in range(PASSES)]
+        x_units = [(0, 0, 512), (0, 512, 512), (1, 0, 512), (1, 512, 512)]
+        x_units = [("x",) + unit for unit in x_units]
+        units = x_units + w_units
+        vector_columns = {("x", 0, 0, 512): 384, ("x", 0, 512, 512): 320, ("x", 1, 512, 512): 256, ("w", 2, 0): 160, ("w", 2, 1): 160, ("w", 3, 1): 96, ("w", 4, 1): 128, ("w", 5, 1): 128}
+        w_codes = [keep.tile([P, PASSES, p[2]], U32, name=f"w_codes{i}", align_bytes=64) for i, p in enumerate(w_parts)]
+        w_scales = [keep.tile([P, PASSES, p[2]], U8, name=f"w_scales{i}", align_bytes=64) for i, p in enumerate(w_parts)]
         raws = []
 
         def load():
-            i = len(raws)
-            if i == len(sources):
+            k = len(raws)
+            if k == len(units):
                 return
-            raw = rawp.tile([P, PACK, sources[i].shape[1]], F32, name="raw")
-            nc.sync.dma_start(out=raw[:], in_=sources[i].rearrange("(p j) n -> p j n", j=PACK))
+            if units[k][0] == "x":
+                g, c0, n = units[k][1:]
+                source = xT[g * K_PASS:(g + 1) * K_PASS, c0:c0 + n]
+            else:
+                i, g = units[k][1:]
+                e, c0, n = w_parts[i]
+                source = w[e, g * K_PASS:(g + 1) * K_PASS, c0:c0 + n]
+            raw = rawp.tile([P, PACK, n], F32, name="raw")
+            nc.sync.dma_start(out=raw[:], in_=source.rearrange("(p j) n -> p j n", j=PACK))
             raws.append(raw)
-            if i == 0:
+            if k == 0:
                 nc.sync.dma_start(offsets[:], offs)
-            if i == len(x_units) + 2:
+            if k == GATE_LOAD:
                 nc.sync.dma_start(out=gates[:], in_=gate[0:P, :])
 
-        def interleave(raw, grouped, vector_columns):
+        def interleave(raw, grouped, vector_part):
             width = raw.shape[2]
-            ends = (0, vector_columns, width)
-            for engine, c0, c1 in zip("vs", ends, ends[1:]):
+            for copy, c0, c1 in ((nc.vector.tensor_copy, 0, vector_part), (nc.scalar.copy, vector_part, width)):
                 if c1 > c0:
-                    dst = grouped[:, c0:c1, :].rearrange("p (c i) j -> p c j i", i=4)
-                    src = raw[:, :, c0:c1].rearrange("p j (c i) -> p c j i", i=4)
-                    if engine == "v":
-                        nc.vector.tensor_copy(out=dst, in_=src)
-                    elif engine == "s":
-                        nc.scalar.copy(out=dst, in_=src)
+                    copy(
+                        out=grouped[:, c0:c1, :].rearrange("p (c i) j -> p c j i", i=4),
+                        in_=raw[:, :, c0:c1].rearrange("p j (c i) -> p c j i", i=4),
+                    )
 
-        def gather_codes(g, h):
-            n = HALF // 16
-            nc.vector.tensor_copy(s_codes[g][h][:], x_codes[g][:].indirect(offsets[:, h * n:(h + 1) * n]))
+        def slots(h):
+            return offsets[:, h * HALF // 16:(h + 1) * HALF // 16]
 
-        def gather_scales(h):
-            n = HALF // 16
-            nc.vector.tensor_copy(s_scales[h][:], x_scales[:].indirect(offsets[:, h * n:(h + 1) * n]))
-
-        def multiply(bank, e, first, w_codes, w_scales, b):
+        def multiply(i):
+            e, c0, n = w_parts[i]
             h, s = divmod(e * C, HALF)
-            for g in range(PASSES):
-                nc.tensor.matmul_mx(
-                    out=bank[:, (e - first) * C:(e - first + 1) * C],
-                    lhsT=w_codes[:, g, b * P:(b + 1) * P].bitcast(FP8X4),
-                    lhsT_scale=w_scales[:, g, b * P:(b + 1) * P],
-                    rhs=s_codes[g][h][:, s:s + C].bitcast(FP8X4),
-                    rhs_scale=s_scales[h][4 * g:P, s:s + C],
-                    start=(g == 0),
-                    stop=(g == PASSES - 1),
-                )
+            banks = []
+            for b in range(n // P):
+                bank = psum.tile([P, C], F32, name=f"bank{c0 // P + b}")
+                for g in range(PASSES):
+                    nc.tensor.matmul_mx(
+                        out=bank[:],
+                        lhsT=w_codes[i][:, g, b * P:(b + 1) * P].bitcast(FP8X4),
+                        lhsT_scale=w_scales[i][:, g, b * P:(b + 1) * P],
+                        rhs=s_codes[g][h][:, s:s + C].bitcast(FP8X4),
+                        rhs_scale=s_scales[h][4 * g:P, s:s + C],
+                        start=(g == 0),
+                        stop=(g == PASSES - 1),
+                    )
+                banks.append(bank)
+            return banks
 
-        def finish(first, count, b, bank):
-            n = count * C
-            y = yp.tile([P, n], F32, name="y")
-            nc.scalar.copy(out=y[:], in_=bank[:, 0:n])
-            o0 = first * COLS_PER_EXPERT
-            nc.vector.tensor_tensor(
-                windows[b][:].indirect(offsets[:, o0:o0 + n // 16]), y[:], gates[:, first * C:first * C + n], MULT
-            )
-            if first + count == E:
-                nc.sync.dma_start(out=out[b * P:(b + 1) * P, :], in_=windows[b][:])
-
-        for i in range(LOADS_AHEAD):
-            load()
-        for i, (g, t0, n, v) in enumerate(x_units):
-            grouped = bfp.tile([P, n, PACK], BF16, tag="grouped", name="x_grouped", align_bytes=64)
-            interleave(raws[i], grouped, v)
-            nc.vector.quantize_mx(
-                out=x_codes[g][:, t0:t0 + n].bitcast(FP8X4),
-                scales=x_scales[4 * g:P, t0:t0 + n],
-                in_=grouped[:].rearrange("p n j -> p (n j)"),
-            )
-            load()
-            if t0 + n == T:
-                gather_codes(g, 0)
-                gather_codes(g, 1)
-        gather_scales(0)
-        gather_scales(1)
-
-        groups = tuple((e, 1) for e in range(E))
-        group_of = {e: (first, count) for first, count in groups for e in range(first, first + count)}
-        vector_columns = {(e, 1): 160 for e in range(1, 7)}
-        banks = {}
-        waiting = []
-        for i, (e, c0, n) in enumerate(w_parts):
-            w_codes = keep.tile([P, PASSES, n], U32, name=f"w_codes{i}", align_bytes=64)
-            w_scales = keep.tile([P, PASSES, n], U8, name=f"w_scales{i}", align_bytes=64)
-            for g in range(PASSES):
-                grouped = bfp.tile([P, n, PACK], BF16, tag="grouped", name="w_grouped", align_bytes=64)
-                interleave(raws[len(x_units) + PASSES * i + g], grouped, vector_columns.get((i, g), 0))
-                nc.vector.quantize_mx(
-                    out=w_codes[:, g, :].bitcast(FP8X4),
-                    scales=w_scales[:, g, :],
-                    in_=grouped[:].rearrange("p n j -> p (n j)"),
-                )
-                load()
-            first, count = group_of[e]
-            ready = waiting
-            waiting = []
+        def finish(i, banks):
+            e, c0, n = w_parts[i]
             for b in range(n // P):
                 block = c0 // P + b
-                if e == first:
-                    banks[block] = psum.tile([P, count * C], F32, name=f"bank{block}")
-                multiply(banks[block], e, first, w_codes, w_scales, b)
-                if e == first + count - 1:
-                    waiting.append((first, count, block, banks[block]))
-            for item in ready:
-                finish(*item)
-        for item in waiting:
+                y = yp.tile([P, C], F32, name="y")
+                nc.scalar.copy(out=y[:], in_=banks[b][:])
+                nc.vector.tensor_tensor(
+                    windows[block][:].indirect(offsets[:, e * C // 16:(e + 1) * C // 16]), y[:], gates[:, e * C:(e + 1) * C], MULT
+                )
+                if e == E - 1:
+                    nc.sync.dma_start(out=out[block * P:(block + 1) * P, :], in_=windows[block][:])
+
+        for k in range(LOADS_AHEAD):
+            load()
+        gathered = False
+        quantised = []
+        multiplied = []
+        for k, unit in enumerate(units):
+            raw = raws[k]
+            grouped = bfp.tile([P, raw.shape[2], PACK], BF16, name="grouped", align_bytes=64)
+            interleave(raw, grouped, vector_columns.get(unit, 0))
+            load()
+            if unit[0] == "x":
+                g, c0, n = unit[1:]
+                codes, scales = x_codes[g][:, c0:c0 + n], x_scales[4 * g:P, c0:c0 + n]
+            else:
+                i, g = unit[1:]
+                codes, scales = w_codes[i][:, g, :], w_scales[i][:, g, :]
+            nc.vector.quantize_mx(out=codes.bitcast(FP8X4), scales=scales, in_=grouped[:].rearrange("p n j -> p (n j)"))
+            if unit[0] == "x" and c0 + n == T:
+                for h in range(2):
+                    nc.vector.tensor_copy(s_codes[g][h][:], x_codes[g][:].indirect(slots(h)))
+                if g == PASSES - 1:
+                    for h in range(2):
+                        nc.vector.tensor_copy(s_scales[h][:], x_scales[:].indirect(slots(h)))
+                    gathered = True
+            if unit[0] == "w" and g == PASSES - 1:
+                quantised.append(i)
+            while gathered and quantised:
+                i = quantised.pop(0)
+                multiplied.append((i, multiply(i)))
+                if len(multiplied) > 2:
+                    finish(*multiplied.pop(0))
+        for item in multiplied:
             finish(*item)

from contextlib import ExitStack

import concourse.mybir as mybir

K, T, E, C, N = 1024, 1024, 8, 128, 512
FLOPS = 2 * E * C * K * N
BYTES = 4 * (K * T + E * K * N + E * C + N * T) + 2 * 128 * (E * C // 16)

F32 = mybir.dt.float32
BF16 = mybir.dt.bfloat16
U32 = mybir.dt.uint32
U16 = mybir.dt.uint16
U8 = mybir.dt.uint8
FP8X4 = mybir.dt.float8_e4m3fn_x4
MULT = mybir.AluOpType.mult

P = 128
PACK = 4
K_PASS = P * PACK
PASSES = K // K_PASS
BLOCKS = N // P
HALF = E * C // 2
LOADS_AHEAD = 10
GATE_LOAD = 6


def tile_routed_moe_kernel(tc, xT, w, gate, offs, out):
    nc = tc.nc
    with ExitStack() as ctx:
        keep = ctx.enter_context(tc.tile_pool(name="keep", bufs=1))
        rawp = ctx.enter_context(tc.tile_pool(name="rawp", bufs=LOADS_AHEAD))
        bfp = ctx.enter_context(tc.tile_pool(name="bfp", bufs=10))
        yp = ctx.enter_context(tc.tile_pool(name="yp", bufs=16))
        psum = ctx.enter_context(tc.psum_pool(name="psum", bufs=2))

        offsets = keep.tile([P, E * C // 16], U16, name="offsets")
        gates = keep.tile([P, E * C], F32, name="gates")
        x_codes = [keep.tile([P, T], U32, name=f"x_codes{g}", align_bytes=64) for g in range(PASSES)]
        x_scales = keep.tile([P, T], U8, name="x_scales", align_bytes=64)
        s_codes = [[keep.tile([P, HALF], U32, name=f"s_codes{g}_{h}", align_bytes=64) for h in range(2)] for g in range(PASSES)]
        s_scales = [keep.tile([P, HALF], U8, name=f"s_scales{h}", align_bytes=64) for h in range(2)]
        windows = [keep.tile([P, T], F32, name=f"window{b}") for b in range(BLOCKS)]

        nc.gpsimd.memset(x_scales[:], 0)

        w_parts = [(e, 0, N) for e in range(E - 1)] + [(E - 1, c, P) for c in range(0, N, P)]
        w_units = [("w", i, g) for i in range(len(w_parts)) for g in range(PASSES)]
        x_units = [(0, 0, 512), (0, 512, 512), (1, 0, 512), (1, 512, 512)]
        x_units = [("x",) + unit for unit in x_units]
        units = x_units + w_units
        vector_columns = {("x", 0, 0, 512): 384, ("x", 0, 512, 512): 320, ("x", 1, 512, 512): 256, ("w", 2, 0): 160, ("w", 2, 1): 160, ("w", 3, 1): 96, ("w", 4, 1): 128, ("w", 5, 1): 128}
        w_codes = [keep.tile([P, PASSES, p[2]], U32, name=f"w_codes{i}", align_bytes=64) for i, p in enumerate(w_parts)]
        w_scales = [keep.tile([P, PASSES, p[2]], U8, name=f"w_scales{i}", align_bytes=64) for i, p in enumerate(w_parts)]
        raws = []

        def load():
            k = len(raws)
            if k == len(units):
                return
            if units[k][0] == "x":
                g, c0, n = units[k][1:]
                source = xT[g * K_PASS:(g + 1) * K_PASS, c0:c0 + n]
            else:
                i, g = units[k][1:]
                e, c0, n = w_parts[i]
                source = w[e, g * K_PASS:(g + 1) * K_PASS, c0:c0 + n]
            raw = rawp.tile([P, PACK, n], F32, name="raw")
            nc.sync.dma_start(out=raw[:], in_=source.rearrange("(p j) n -> p j n", j=PACK))
            raws.append(raw)
            if k == 0:
                nc.sync.dma_start(offsets[:], offs)
            if k == GATE_LOAD:
                nc.sync.dma_start(out=gates[:], in_=gate[0:P, :])

        def interleave(raw, grouped, vector_part):
            width = raw.shape[2]
            for copy, c0, c1 in ((nc.vector.tensor_copy, 0, vector_part), (nc.scalar.copy, vector_part, width)):
                if c1 > c0:
                    copy(
                        out=grouped[:, c0:c1, :].rearrange("p (c i) j -> p c j i", i=4),
                        in_=raw[:, :, c0:c1].rearrange("p j (c i) -> p c j i", i=4),
                    )

        def slots(h):
            return offsets[:, h * HALF // 16:(h + 1) * HALF // 16]

        def multiply(i):
            e, c0, n = w_parts[i]
            h, s = divmod(e * C, HALF)
            banks = []
            for b in range(n // P):
                bank = psum.tile([P, C], F32, name=f"bank{c0 // P + b}")
                for g in range(PASSES):
                    nc.tensor.matmul_mx(
                        out=bank[:],
                        lhsT=w_codes[i][:, g, b * P:(b + 1) * P].bitcast(FP8X4),
                        lhsT_scale=w_scales[i][:, g, b * P:(b + 1) * P],
                        rhs=s_codes[g][h][:, s:s + C].bitcast(FP8X4),
                        rhs_scale=s_scales[h][4 * g:P, s:s + C],
                        start=(g == 0),
                        stop=(g == PASSES - 1),
                    )
                banks.append(bank)
            return banks

        def finish(i, banks):
            e, c0, n = w_parts[i]
            for b in range(n // P):
                block = c0 // P + b
                y = yp.tile([P, C], F32, name="y")
                nc.scalar.copy(out=y[:], in_=banks[b][:])
                nc.vector.tensor_tensor(
                    windows[block][:].indirect(offsets[:, e * C // 16:(e + 1) * C // 16]), y[:], gates[:, e * C:(e + 1) * C], MULT
                )
                if e == E - 1:
                    nc.sync.dma_start(out=out[block * P:(block + 1) * P, :], in_=windows[block][:])

        for k in range(LOADS_AHEAD):
            load()
        gathered = False
        quantised = []
        multiplied = []
        for k, unit in enumerate(units):
            raw = raws[k]
            grouped = bfp.tile([P, raw.shape[2], PACK], BF16, name="grouped", align_bytes=64)
            interleave(raw, grouped, vector_columns.get(unit, 0))
            load()
            if unit[0] == "x":
                g, c0, n = unit[1:]
                codes, scales = x_codes[g][:, c0:c0 + n], x_scales[4 * g:P, c0:c0 + n]
            else:
                i, g = unit[1:]
                codes, scales = w_codes[i][:, g, :], w_scales[i][:, g, :]
            nc.vector.quantize_mx(out=codes.bitcast(FP8X4), scales=scales, in_=grouped[:].rearrange("p n j -> p (n j)"))
            if unit[0] == "x" and c0 + n == T:
                for h in range(2):
                    nc.vector.tensor_copy(s_codes[g][h][:], x_codes[g][:].indirect(slots(h)))
                if g == PASSES - 1:
                    for h in range(2):
                        nc.vector.tensor_copy(s_scales[h][:], x_scales[:].indirect(slots(h)))
                    gathered = True
            if unit[0] == "w" and g == PASSES - 1:
                quantised.append(i)
            while gathered and quantised:
                i = quantised.pop(0)
                multiplied.append((i, multiply(i)))
                if len(multiplied) > 2:
                    finish(*multiplied.pop(0))
        for item in multiplied:
            finish(*item)
